import numpy as np
import ml_dtypes


def mxq(x, axis, fmt="e4m3"):
    dtype, down = {"e4m3": (ml_dtypes.float8_e4m3fn, 7), "e5m2": (ml_dtypes.float8_e5m2, 14)}[fmt]
    v = np.moveaxis(np.asarray(x, np.float32).astype(ml_dtypes.bfloat16).astype(np.float64), axis, -1)
    blocks = v.reshape(v.shape[:-1] + (-1, 32))
    amax = np.abs(blocks).max(-1, keepdims=True)
    byte = np.maximum(np.where(amax > 0, np.frexp(amax)[1] - 1 + 127, 0) - down, 1)
    scale = np.exp2(byte - 127.0)
    codes = (blocks / scale).astype(np.float32).astype(dtype).astype(np.float64)
    return np.moveaxis((codes * scale).reshape(v.shape), -1, axis)


WIDE = False


def mx_kscale(k):
    if not WIDE:
        return np.ones(k)
    levels = np.array([10, -10, 5, -5, 0])
    if k % 512:
        return np.exp2(np.random.permutation(np.resize(levels, k // 32))).repeat(32)
    a = np.empty((k // 512, 16))
    for p in range(k // 512):
        a[p, :8] = np.random.permutation(np.resize(levels, 8))
        for g in range(8):
            far = levels[np.abs(levels - a[p, g]) >= 10]
            a[p, g + 8] = far[np.random.randint(len(far))]
    return np.exp2(a.ravel()).repeat(32)


BF16 = ml_dtypes.bfloat16


def bf(x):
    return np.asarray(x, np.float32).astype(BF16)


def f64(x):
    return np.asarray(x).astype(np.float64)

def planes(Y):
    n, m = Y.shape
    b = f64(bf(Y)).reshape(n // 32, 32, m)
    amax = np.abs(b).max(1)
    byte = np.clip(np.where(amax > 0, np.frexp(amax)[1] - 1 + 127 - 7, 1), 1, 254)
    codes = (b * np.exp2(127.0 - byte)[:, None, :]).reshape(n, m).astype(np.float32).astype(ml_dtypes.float8_e4m3fn).view(np.uint8)
    words = codes.reshape(n // 512, 128, 4, m).transpose(0, 1, 3, 2)
    return np.ascontiguousarray(words), np.ascontiguousarray(byte.astype(np.uint8).reshape(n // 512, 16, m))


N, M, D, E, P = 1024, 1024, 1024, 512, 1024


def exp_kernel(a, b):
    scale = np.sqrt(a.shape[-1])
    return np.exp((mxq(a, 1, "e4m3") @ mxq(b.T, 0, "e4m3")) / scale)


def double_centre(l):
    mr = np.mean(l, axis=1)
    mc = np.mean(l, axis=0)
    mm = np.mean(mr)
    return l - mr[:, None] - mc[None, :] + mm


def setup_inputs():
    s, g, t = mx_kscale(D), mx_kscale(E), mx_kscale(M)
    y = 0.8 * np.random.standard_normal((N, E)) + 0.3 * np.random.standard_normal((1, E))
    v = 0.8 * np.random.standard_normal((M, E)) + 0.3 * np.random.standard_normal((1, E))
    return {
        "x": bf(np.random.standard_normal((N, D)) * 0.8 * s),
        "u": bf(np.random.standard_normal((M, D)) * 0.8 / s),
        "y": bf(y * g),
        "v": bf(v / g),
        "r": bf((1.0 + 0.1 * np.random.standard_normal(M)) * t),
        "z": bf(np.random.standard_normal((M, P)) / t[:, None]),
    }


def core(x, u, y, v, r, z):
    k = exp_kernel(f64(x), f64(u))
    l = exp_kernel(f64(y), f64(v))
    lc = double_centre(l)
    a = k * lc * f64(r)[None, :]
    return (mxq(a, 1, "e4m3") @ mxq(f64(z), 0, "e4m3")) / np.sqrt(z.shape[0])


def reference(x, u, y, v, r, z):
    R_out = core(x, u, y, v, r, z)
    words, scales = planes(R_out)
    return R_out, words, scales

@@ -1,0 +1,366 @@
+import math
+from contextlib import ExitStack
+
+import concourse.mybir as mybir
+from concourse.masks import make_identity
+
+N, M, D, E, PCOLS = 1024, 1024, 1024, 512, 1024
+FLOPS = 2 * N * M * (D + E + PCOLS)
+
+F32 = mybir.dt.float32
+BF16 = mybir.dt.bfloat16
+U32 = mybir.dt.uint32
+I32 = mybir.dt.int32
+U8 = mybir.dt.uint8
+FP8X4 = mybir.dt.float8_e4m3fn_x4
+ALU = mybir.AluOpType
+ACT = mybir.ActivationFunctionType
+AX = mybir.AxisListType
+
+P = 128
+PACK = 4
+GROUP = P * PACK
+
+
+def tile_hsicexpkernelgrad_x1_kernel(tc, x, u, y, v, r, z, out_0, out_1, out_2):
+    nc = tc.nc
+    with ExitStack() as ctx:
+        const = ctx.enter_context(tc.tile_pool(name="const", bufs=1))
+        raw = ctx.enter_context(tc.tile_pool(name="raw", bufs=1))
+        grp = ctx.enter_context(tc.tile_pool(name="grp", bufs=1))
+        codes = ctx.enter_context(tc.tile_pool(name="codes", bufs=1))
+        big = ctx.enter_context(tc.tile_pool(name="big", bufs=1))
+        psum = ctx.enter_context(tc.psum_pool(name="psum", bufs=1))
+        ctx.enter_context(tc.manual_schedule())
+
+        ident = const.tile([P, P], F32, name="ident")
+        make_identity(nc, ident[:])
+        ones_mean = const.tile([P, P], F32, name="ones_mean")
+        nc.gpsimd.memset(ones_mean[:], 1.0 / 1024)
+        ones_grand = const.tile([P, P], F32, name="ones_grand")
+        nc.gpsimd.memset(ones_grand[:], 1.0 / (1024 * 1024))
+        warm = const.tile([P, 1], F32, name="warm")
+        nc.vector.memset(warm[:], 0.0)
+        warm_out = const.tile([P, 1], F32, name="warm_out")
+        nc.scalar.activation(out=warm_out[:], in_=warm[:], func=ACT.Exp)
+        r_bf = const.tile([P, 2, PACK], BF16, name="r_bf")
+        nc.gpsimd.dma_start(out=r_bf[:], in_=r.rearrange("(g p t) -> p g t", p=P, t=PACK))
+        r_sb = const.tile([P, 8], F32, name="r_sb")
+        nc.gpsimd.tensor_copy(out=r_sb[:], in_=r_bf[:].rearrange("p g t -> p (g t)"))
+        sums = const.tile([P, 2, 8], F32, name="sums")
+
+        raws = {}
+
+        def load_rows(name, src, g, pieces):
+            k_len = src.shape[1]
+            t_ = raw.tile([P, PACK, k_len], BF16, name="raw_%s%d" % (name, g), tag="short" if k_len == E else "wide", bufs=4 if k_len == E else 6)
+            rows = src[g * GROUP:(g + 1) * GROUP, :].rearrange("(m t) k -> m t k", t=PACK)
+            w = PACK // pieces
+            for b in range(pieces):
+                nc.sync.dma_start(out=t_[:, b * w:(b + 1) * w, :], in_=rows[:, b * w:(b + 1) * w, :])
+            raws[name, g] = t_
+
+        load_rows("y", y, 0, 2)
+        load_rows("v", v, 0, 1)
+        load_rows("v", v, 1, 1)
+        load_rows("y", y, 1, 1)
+        load_rows("u", u, 0, 2)
+        load_rows("u", u, 1, 2)
+        load_rows("x", x, 0, 2)
+        load_rows("z", z, 0, 2)
+        load_rows("z", z, 1, 2)
+        load_rows("x", x, 1, 2)
+
+        turn_ring = [0, 1, 2, 3, 4]
+        acc_ring = [5, 6, 7]
+        out_ring = [0, 1, 2, 5, 6, 7, 3, 4]
+
+        def next_bank(ring):
+            i = ring[0]
+            ring.remove(i)
+            ring.append(i)
+            return psum.tile([P, GROUP], F32, name="bank", tag="bank%d" % i)
+
+        def turn_bank():
+            return next_bank(turn_ring)[:].rearrange("p (a e r) -> p a e r", a=2, e=2)
+
+        code = {}
+        plane = {}
+        grouped = {}
+
+        def turn(name, g, h, b):
+            words = raws[name, g][:].rearrange("m t k -> m (t k)").bitcast(F32)
+            per_row = (E if name in "yv" else D) // 2
+            bank = turn_bank()
+            for a in range(2):
+                base = (2 * b + a) * per_row + 256 * h
+                for e in range(2):
+                    nc.tensor.transpose(bank[:, a, e, :], words[:, base + e:base + 256:2], ident[:])
+            return bank
+
+        def copy_out(bank, name, g, h, b, eng):
+            key = (name, g, h)
+            if key not in grouped:
+                grouped[key] = grp.tile([P, GROUP, PACK], BF16, name="grouped", tag="grouped", bufs=6, align_bytes=64)
+            dst = grouped[key][:].rearrange("p r k -> p (r k)").bitcast(F32)
+            dst = dst.rearrange("p (b a r e) -> p b a r e", b=2, a=2, e=2)[:, b]
+            src = bank.rearrange("p a e r -> p a r e")
+            if eng == "V":
+                nc.vector.tensor_copy(out=dst, in_=src)
+            else:
+                nc.scalar.copy(out=dst, in_=src)
+
+        def quantize(key, src):
+            c_ = codes.tile([P, GROUP], U32, name="c_%s%d%d" % key, align_bytes=64)
+            s_ = codes.tile([P, GROUP], U8, name="s_%s%d%d" % key, align_bytes=64)
+            nc.vector.quantize_mx(out=c_[:].bitcast(FP8X4), scales=s_[:], in_=src[:].rearrange("p r k -> p (r k)"))
+            code[key] = c_
+            plane[key] = s_
+
+        def mx(bank, lkey, lcols, rkey, rcols, start, stop):
+            nc.tensor.matmul_mx(
+                out=bank[:], lhsT=code[lkey][:, lcols].bitcast(FP8X4), lhsT_scale=plane[lkey][:, lcols],
+                rhs=code[rkey][:, rcols].bitcast(FP8X4), rhs_scale=plane[rkey][:, rcols], start=start, stop=stop)
+
+        full = slice(0, GROUP)
+
+        l_sb = [big.tile([P, 8, GROUP], F32, name="l_sb%d" % ih) for ih in range(2)]
+        k_sb = [big.tile([P, 8, GROUP], F32, name="k_sb%d" % ih) for ih in range(2)]
+        pair = [big.tile([P, 4, GROUP], F32, name="pair%d" % ih) for ih in range(2)]
+
+        def acc_bank():
+            return next_bank(acc_ring)
+
+        def l_mm(jt, ih):
+            g, t = divmod(jt, 4)
+            bank = acc_bank()
+            mx(bank, ("v", g, 0), slice(t * P, (t + 1) * P), ("y", ih, 0), full, True, True)
+            return bank
+
+        def l_exp(bank, jt, ih):
+            nc.scalar.activation(out=l_sb[ih][:, jt, :], in_=bank[:], func=ACT.Exp, scale=1.0 / math.sqrt(E),
+                                 accum_out=sums[:, ih, jt:jt + 1])
+
+        def pair_add(q, ih):
+            nc.vector.tensor_tensor(out=pair[ih][:, q, :], in0=l_sb[ih][:, 2 * q, :], in1=l_sb[ih][:, 2 * q + 1, :], op=ALU.add)
+
+        def k_mm(jt, ih):
+            g, t = divmod(jt, 4)
+            bank = acc_bank()
+            for h in range(2):
+                mx(bank, ("u", g, h), slice(t * P, (t + 1) * P), ("x", ih, h), full, h == 0, h == 1)
+            return bank
+
+        def k_exp(bank, jt, ih):
+            nc.scalar.activation(out=k_sb[ih][:, jt, :], in_=bank[:], func=ACT.Exp, scale=1.0 / math.sqrt(D))
+
+        def k_r(jt, ih):
+            nc.gpsimd.tensor_scalar(out=k_sb[ih][:, jt, :], in0=k_sb[ih][:, jt, :], scalar1=r_sb[:, jt:jt + 1], scalar2=0.0,
+                                    op0=ALU.mult, op1=ALU.add)
+
+        mean = {}
+
+        def mean_mm(ih):
+            mean[ih] = psum.tile([P, GROUP], F32, name="mean", tag="bank%d" % (3 + ih))
+            for q in range(0, 4, 2):
+                nc.tensor.matmul(mean[ih][:], lhsT=ones_mean[:], rhs=pair[ih][:, q, :], start=q == 0, stop=q == 2)
+
+        def quad_add(q, ih):
+            nc.gpsimd.tensor_tensor(out=pair[ih][:, 2 * q, :], in0=pair[ih][:, 2 * q, :], in1=pair[ih][:, 2 * q + 1, :], op=ALU.add)
+
+        shift = const.tile([P, 8], F32, name="shift")
+
+        def column_means():
+            col = const.tile([P, 8], F32, name="col")
+            nc.vector.tensor_tensor(out=col[:], in0=sums[:, 0, :], in1=sums[:, 1, :], op=ALU.add)
+            tot = const.tile([P, 1], F32, name="tot")
+            nc.vector.reduce_sum(out=tot[:], in_=col[:], axis=AX.X)
+            bank = next_bank(acc_ring)
+            grand = bank[:, 0:1]
+            nc.tensor.matmul(grand, lhsT=ones_grand[:], rhs=tot[:], start=True, stop=True)
+            nc.vector.tensor_scalar(out=shift[:], in0=col[:], scalar1=-1.0 / 1024, scalar2=grand, op0=ALU.mult, op1=ALU.add)
+
+        def centre(jt, ih):
+            nc.vector.scalar_tensor_tensor(out=l_sb[ih][:, jt, :], in0=l_sb[ih][:, jt, :], scalar=shift[:, jt:jt + 1],
+                                           in1=mean[ih][:], op0=ALU.add, op1=ALU.subtract)
+
+        def product(jg, ih, part, parts):
+            key = ("a", jg, ih)
+            if key not in grouped:
+                grouped[key] = grp.tile([P, GROUP, PACK], BF16, name="grouped", tag="grouped", bufs=6, align_bytes=64)
+            w = GROUP // parts
+            cols = slice(part * w, (part + 1) * w)
+            nc.vector.tensor_tensor(
+                out=grouped[key][:, part * w:(part + 1) * w, :],
+                in0=l_sb[ih][:, 4 * jg:4 * jg + 4, cols].rearrange("p t i -> p i t"),
+                in1=k_sb[ih][:, 4 * jg:4 * jg + 4, cols].rearrange("p t i -> p i t"), op=ALU.mult)
+
+        def z_interleave(g, n, eng):
+            key = ("z", g, n)
+            grouped[key] = grp.tile([P, GROUP, PACK], BF16, name="grouped", tag="grouped", bufs=6, align_bytes=64)
+            dst = grouped[key][:].rearrange("p (c i) t -> p c t i", i=4)
+            src = raws["z", g][:, :, n * GROUP:(n + 1) * GROUP].rearrange("p t (c i) -> p c t i", i=4)
+            if eng == "V":
+                nc.vector.tensor_copy(out=dst, in_=src)
+            else:
+                nc.scalar.copy(out=dst, in_=src)
+
+        def q_(key):
+            quantize(key, grouped[key])
+
+        res = {}
+        resg = {}
+
+        def out_mm(ih, n, t):
+            flat = next_bank(out_ring)[:]
+            for g in range(2):
+                nc.tensor.matmul_mx(
+                    out=flat, lhsT=code["a", g, ih][:, t * P:(t + 1) * P].bitcast(FP8X4), lhsT_scale=plane["a", g, ih][:, t * P:(t + 1) * P],
+                    rhs=code["z", g, n][:].bitcast(FP8X4), rhs_scale=plane["z", g, n][:], start=g == 0, stop=g == 1)
+            return flat
+
+        def out_copy(flat, ih, n, t, eng):
+            if (ih, n) not in res:
+                res[ih, n] = raw.tile([P, PACK, GROUP], F32, name="res", tag="wide", bufs=6)
+            dst = res[ih, n][:, t, :]
+            if eng == "V":
+                nc.vector.tensor_scalar(out=dst, in0=flat, scalar1=1.0 / 32, scalar2=None, op0=ALU.mult)
+            else:
+                nc.scalar.activation(out=dst, in_=flat, func=ACT.Copy, scale=1.0 / 32)
+
+        def out_store(ih, n, ts):
+            nc.sync.dma_start(
+                out=out_0[ih * GROUP:(ih + 1) * GROUP, n * GROUP:(n + 1) * GROUP].rearrange("(m t) p -> m t p", t=PACK)[:, ts, :],
+                in_=res[ih, n][:, ts, :])
+
+        o_codes = [codes.tile([P, PCOLS], U32, name="o_codes%d" % ih, align_bytes=64) for ih in range(2)]
+        o_plane = [codes.tile([P, PCOLS], U8, name="o_plane%d" % ih, align_bytes=64) for ih in range(2)]
+
+        def out_round(ih, n, part=0, parts=1):
+            w = GROUP // parts
+            cols = slice(part * w, (part + 1) * w)
+            key = ("o", ih, n)
+            if key not in grouped:
+                grouped[key] = grp.tile([P, GROUP, PACK], BF16, name="grouped", tag="grouped", bufs=6, align_bytes=64)
+            nc.vector.tensor_copy(out=grouped[key][:, cols, :], in_=res[ih, n][:, :, cols].rearrange("p t n -> p n t"))
+
+        def out_quant(ih, n, part=0, parts=1):
+            w = GROUP // parts
+            cols = slice(part * w, (part + 1) * w)
+            gcols = slice(n * GROUP + part * w, n * GROUP + (part + 1) * w)
+            nc.vector.quantize_mx(out=o_codes[ih][:, gcols].bitcast(FP8X4), scales=o_plane[ih][:, gcols],
+                                  in_=grouped["o", ih, n][:, cols, :].rearrange("p n t -> p (n t)"))
+
+        def words_store(ih, first, last):
+            nc.sync.dma_start(out=out_1[ih][:, first:last, :].rearrange("p n t -> p (n t)").bitcast(I32),
+                              in_=o_codes[ih][:, first:last].bitcast(I32))
+
+        def plane_store(ih):
+            for q in range(4):
+                nc.sync.dma_start(out=out_2[ih, 4 * q:4 * q + 4, :].bitcast(I32), in_=o_plane[ih][32 * q:32 * q + 4, :].bitcast(I32))
+
+        def prep(name, g, h, engs):
+            for b in range(2):
+                copy_out(turn(name, g, h, b), name, g, h, b, engs[b])
+
+        prep("y", 0, 0, "VS")
+        q_(("y", 0, 0))
+        prep("v", 0, 0, "VS")
+        q_(("v", 0, 0))
+        prep("v", 1, 0, "VS")
+        for jt in range(4):
+            l_exp(l_mm(jt, 0), jt, 0)
+        q_(("v", 1, 0))
+        prep("y", 1, 0, "VV")
+        for jt in range(4, 8):
+            l_exp(l_mm(jt, 0), jt, 0)
+        q_(("y", 1, 0))
+        pair_add(0, 0)
+        pair_add(1, 0)
+        quad_add(0, 0)
+        for s in range(4):
+            g, h = divmod(s, 2)
+            for jt in (2 * s, 2 * s + 1):
+                l_exp(l_mm(jt, 1), jt, 1)
+            prep("u", g, h, "VS")
+            if s < 2:
+                pair_add(2 + s, 0)
+            if s == 1:
+                quad_add(1, 0)
+            q_(("u", g, h))
+            pair_add(s, 1)
+            if s % 2:
+                quad_add(s // 2, 1)
+        prep("x", 0, 0, "SS")
+        prep("x", 0, 1, "SS")
+        for h in range(2):
+            q_(("x", 0, h))
+        prep("x", 1, 0, "SS")
+        z_interleave(0, 0, "V")
+        mean_mm(0)
+        column_means()
+        for jt in range(8):
+            k_exp(k_mm(jt, 0), jt, 0)
+            k_r(jt, 0)
+            centre(jt, 0)
+            if jt == 3:
+                prep("x", 1, 1, "SS")
+                q_(("z", 0, 0))
+                q_(("x", 1, 0))
+        for n_ in (3, 4):
+            turn_ring.remove(n_)
+        mean_mm(1)
+        q_(("x", 1, 1))
+        z_interleave(1, 0, "S")
+        product(0, 0, 0, 2)
+        product(0, 0, 1, 2)
+        product(1, 0, 0, 2)
+        q_(("a", 0, 0))
+        product(1, 0, 1, 2)
+        q_(("z", 1, 0))
+        for jt in range(8):
+            k_exp(k_mm(jt, 1), jt, 1)
+            k_r(jt, 1)
+            centre(jt, 1)
+            if jt == 0:
+                q_(("a", 1, 0))
+        z_interleave(0, 1, "S")
+        product(0, 1, 0, 2)
+        for t in range(4):
+            out_copy(out_mm(0, 0, t), 0, 0, t, "S")
+        out_store(0, 0, slice(0, 4))
+        z_interleave(1, 1, "S")
+        q_(("z", 0, 1))
+        product(0, 1, 1, 2)
+        product(1, 1, 0, 2)
+        q_(("a", 0, 1))
+        q_(("z", 1, 1))
+        product(1, 1, 1, 2)
+        out_round(0, 0)
+        q_(("a", 1, 1))
+        for t in range(4):
+            out_copy(out_mm(0, 1, t), 0, 1, t, "S")
+        out_store(0, 1, slice(0, 4))
+        for t in range(4):
+            out_copy(out_mm(1, 0, t), 1, 0, t, "S")
+            if t % 2:
+                out_store(1, 0, slice(t - 1, t + 1))
+        out_round(0, 1)
+        out_quant(0, 0)
+        words_store(0, 0, 512)
+        out_quant(0, 1)
+        words_store(0, 512, 1024)
+        plane_store(0)
+        out_round(1, 0)
+        for t in range(4):
+            out_copy(out_mm(1, 1, t), 1, 1, t, "S")
+            if t % 2:
+                out_store(1, 1, slice(t - 1, t + 1))
+        out_quant(1, 0)
+        words_store(1, 0, 512)
+        out_round(1, 1, 0, 2)
+        out_round(1, 1, 1, 2)
+        out_quant(1, 1, 0, 2)
+        out_quant(1, 1, 1, 2)
+        words_store(1, 512, 1024)
+        plane_store(1)

@@ -31,7 +31,6 @@ def tile_hsicexpkernelgrad_x1_kernel(tc, x, u, y, v, r, z, out_0, out_1, out_2):
         codes = ctx.enter_context(tc.tile_pool(name="codes", bufs=1))
         big = ctx.enter_context(tc.tile_pool(name="big", bufs=1))
         psum = ctx.enter_context(tc.psum_pool(name="psum", bufs=1))
-        ctx.enter_context(tc.manual_schedule())
 
         ident = const.tile([P, P], F32, name="ident")
         make_identity(nc, ident[:])
@@ -39,6 +38,8 @@ def tile_hsicexpkernelgrad_x1_kernel(tc, x, u, y, v, r, z, out_0, out_1, out_2):
         nc.gpsimd.memset(ones_mean[:], 1.0 / 1024)
         ones_grand = const.tile([P, P], F32, name="ones_grand")
         nc.gpsimd.memset(ones_grand[:], 1.0 / (1024 * 1024))
+        dummy = const.tile([P, GROUP], BF16, name="dummy")
+        nc.vector.memset(dummy[:], 0.0)
         warm = const.tile([P, 1], F32, name="warm")
         nc.vector.memset(warm[:], 0.0)
         warm_out = const.tile([P, 1], F32, name="warm_out")
@@ -154,11 +155,19 @@ def tile_hsicexpkernelgrad_x1_kernel(tc, x, u, y, v, r, z, out_0, out_1, out_2):
         def k_exp(bank, jt, ih):
             nc.scalar.activation(out=k_sb[ih][:, jt, :], in_=bank[:], func=ACT.Exp, scale=1.0 / math.sqrt(D))
 
-        def k_r(jt, ih):
-            nc.gpsimd.tensor_scalar(out=k_sb[ih][:, jt, :], in0=k_sb[ih][:, jt, :], scalar1=r_sb[:, jt:jt + 1], scalar2=0.0,
+        def k_r(jt, ih, eng):
+            if eng == "S":
+                nc.scalar.activation(out=k_sb[ih][:, jt, :], in_=k_sb[ih][:, jt, :], func=ACT.Copy, scale=r_sb[:, jt:jt + 1])
+                return
+            (nc.gpsimd if eng == "G" else nc.vector).tensor_scalar(out=k_sb[ih][:, jt, :], in0=k_sb[ih][:, jt, :], scalar1=r_sb[:, jt:jt + 1], scalar2=0.0,
                                     op0=ALU.mult, op1=ALU.add)
 
         mean = {}
+
+        def keep_warm(count):
+            bank = psum.tile([P, GROUP], F32, name="bank", tag="bank7")
+            for i in range(count):
+                nc.tensor.matmul(bank[:], lhsT=dummy[:, 0:P], rhs=dummy[:], start=True, stop=True)
 
         def mean_mm(ih):
             mean[ih] = psum.tile([P, GROUP], F32, name="mean", tag="bank%d" % (3 + ih))
@@ -166,7 +175,7 @@ def tile_hsicexpkernelgrad_x1_kernel(tc, x, u, y, v, r, z, out_0, out_1, out_2):
                 nc.tensor.matmul(mean[ih][:], lhsT=ones_mean[:], rhs=pair[ih][:, q, :], start=q == 0, stop=q == 2)
 
         def quad_add(q, ih):
-            nc.gpsimd.tensor_tensor(out=pair[ih][:, 2 * q, :], in0=pair[ih][:, 2 * q, :], in1=pair[ih][:, 2 * q + 1, :], op=ALU.add)
+            nc.vector.tensor_tensor(out=pair[ih][:, 2 * q, :], in0=pair[ih][:, 2 * q, :], in1=pair[ih][:, 2 * q + 1, :], op=ALU.add)
 
         shift = const.tile([P, 8], F32, name="shift")
 
@@ -191,9 +200,9 @@ def tile_hsicexpkernelgrad_x1_kernel(tc, x, u, y, v, r, z, out_0, out_1, out_2):
             w = GROUP // parts
             cols = slice(part * w, (part + 1) * w)
             nc.vector.tensor_tensor(
-                out=grouped[key][:, part * w:(part + 1) * w, :],
-                in0=l_sb[ih][:, 4 * jg:4 * jg + 4, cols].rearrange("p t i -> p i t"),
-                in1=k_sb[ih][:, 4 * jg:4 * jg + 4, cols].rearrange("p t i -> p i t"), op=ALU.mult)
+                out=grouped[key][:, cols, :].rearrange("p (c i) t -> p c t i", i=4),
+                in0=l_sb[ih][:, 4 * jg:4 * jg + 4, cols].rearrange("p t (c i) -> p c t i", i=4),
+                in1=k_sb[ih][:, 4 * jg:4 * jg + 4, cols].rearrange("p t (c i) -> p c t i", i=4), op=ALU.mult)
 
         def z_interleave(g, n, eng):
             key = ("z", g, n)
@@ -236,13 +245,15 @@ def tile_hsicexpkernelgrad_x1_kernel(tc, x, u, y, v, r, z, out_0, out_1, out_2):
         o_codes = [codes.tile([P, PCOLS], U32, name="o_codes%d" % ih, align_bytes=64) for ih in range(2)]
         o_plane = [codes.tile([P, PCOLS], U8, name="o_plane%d" % ih, align_bytes=64) for ih in range(2)]
 
-        def out_round(ih, n, part=0, parts=1):
+        def out_round(ih, n, eng="V", part=0, parts=1):
             w = GROUP // parts
             cols = slice(part * w, (part + 1) * w)
             key = ("o", ih, n)
             if key not in grouped:
                 grouped[key] = grp.tile([P, GROUP, PACK], BF16, name="grouped", tag="grouped", bufs=6, align_bytes=64)
-            nc.vector.tensor_copy(out=grouped[key][:, cols, :], in_=res[ih, n][:, :, cols].rearrange("p t n -> p n t"))
+            (nc.scalar.copy if eng == "S" else nc.vector.tensor_copy)(
+                out=grouped[key][:, cols, :].rearrange("p (c i) t -> p c t i", i=4),
+                in_=res[ih, n][:, :, cols].rearrange("p t (c i) -> p c t i", i=4))
 
         def out_quant(ih, n, part=0, parts=1):
             w = GROUP // parts
@@ -263,9 +274,12 @@ def tile_hsicexpkernelgrad_x1_kernel(tc, x, u, y, v, r, z, out_0, out_1, out_2):
             for b in range(2):
                 copy_out(turn(name, g, h, b), name, g, h, b, engs[b])
 
+        keep_warm(5)
         prep("y", 0, 0, "VS")
+        keep_warm(2)
         q_(("y", 0, 0))
         prep("v", 0, 0, "VS")
+        keep_warm(2)
         q_(("v", 0, 0))
         prep("v", 1, 0, "VS")
         for jt in range(4):
@@ -277,7 +291,6 @@ def tile_hsicexpkernelgrad_x1_kernel(tc, x, u, y, v, r, z, out_0, out_1, out_2):
         q_(("y", 1, 0))
         pair_add(0, 0)
         pair_add(1, 0)
-        quad_add(0, 0)
         for s in range(4):
             g, h = divmod(s, 2)
             for jt in (2 * s, 2 * s + 1):
@@ -285,32 +298,35 @@ def tile_hsicexpkernelgrad_x1_kernel(tc, x, u, y, v, r, z, out_0, out_1, out_2):
             prep("u", g, h, "VS")
             if s < 2:
                 pair_add(2 + s, 0)
+            q_(("u", g, h))
+            quad_add(0, 0) if s == 0 else None
+            pair_add(s, 1)
             if s == 1:
                 quad_add(1, 0)
-            q_(("u", g, h))
-            pair_add(s, 1)
-            if s % 2:
-                quad_add(s // 2, 1)
+            if s == 2:
+                quad_add(0, 1)
         prep("x", 0, 0, "SS")
         prep("x", 0, 1, "SS")
-        for h in range(2):
-            q_(("x", 0, h))
-        prep("x", 1, 0, "SS")
-        z_interleave(0, 0, "V")
+        q_(("x", 0, 0))
+        quad_add(1, 1)
+        q_(("x", 0, 1))
         mean_mm(0)
+        z_interleave(0, 0, "V")
         column_means()
         for jt in range(8):
             k_exp(k_mm(jt, 0), jt, 0)
-            k_r(jt, 0)
+            k_r(jt, 0, "G")
             centre(jt, 0)
-            if jt == 3:
-                prep("x", 1, 1, "SS")
-                q_(("z", 0, 0))
+            if jt in (2, 5):
+                h = jt // 3
+                prep("x", 1, h, "SS")
+            if jt == 5:
                 q_(("x", 1, 0))
+        q_(("z", 0, 0))
+        q_(("x", 1, 1))
         for n_ in (3, 4):
             turn_ring.remove(n_)
         mean_mm(1)
-        q_(("x", 1, 1))
         z_interleave(1, 0, "S")
         product(0, 0, 0, 2)
         product(0, 0, 1, 2)
@@ -320,7 +336,7 @@ def tile_hsicexpkernelgrad_x1_kernel(tc, x, u, y, v, r, z, out_0, out_1, out_2):
         q_(("z", 1, 0))
         for jt in range(8):
             k_exp(k_mm(jt, 1), jt, 1)
-            k_r(jt, 1)
+            k_r(jt, 1, "S")
             centre(jt, 1)
             if jt == 0:
                 q_(("a", 1, 0))
@@ -358,8 +374,8 @@ def tile_hsicexpkernelgrad_x1_kernel(tc, x, u, y, v, r, z, out_0, out_1, out_2):
                 out_store(1, 1, slice(t - 1, t + 1))
         out_quant(1, 0)
         words_store(1, 0, 512)
-        out_round(1, 1, 0, 2)
-        out_round(1, 1, 1, 2)
+        out_round(1, 1, "V", 0, 2)
+        out_round(1, 1, "V", 1, 2)
         out_quant(1, 1, 0, 2)
         out_quant(1, 1, 1, 2)
         words_store(1, 512, 1024)

@@ -4,8 +4,8 @@ from contextlib import ExitStack
 import concourse.mybir as mybir
 from concourse.masks import make_identity
 
-N, M, D, E, PCOLS = 1024, 1024, 1024, 512, 1024
-FLOPS = 2 * N * M * (D + E + PCOLS)
+N, M, D, E, COLS = 1024, 1024, 1024, 512, 1024
+FLOPS = 2 * N * M * (D + E + COLS)
 
 F32 = mybir.dt.float32
 BF16 = mybir.dt.bfloat16
@@ -20,363 +20,270 @@ AX = mybir.AxisListType
 P = 128
 PACK = 4
 GROUP = P * PACK
+TILES = 8
+HALF = GROUP // 2
+HEAD_WARMERS = 5
+
+LOADS = "y0a y0b v0a v0b v1 y1 u0a u0b z0a z0b u1a u1b x0a x0b x1a x1b z1a z1b"
+
+ORDER = """
+warmturn.y.0.0.0.0 turn.y.0.0.1.1 copy.y.0.0.0.S.4 turn.v.0.0.0.2 copy.y.0.0.1.S.4 turn.v.0.0.1.3 copy.v.0.0.0.V.5
+turn.v.1.0.0.4 copy.v.0.0.1.V.5 turn.v.1.0.1.5 quant.y.0.0 turn.y.1.0.1.6 quant.v.0.0 copy.v.1.0.1.S.6 turn.y.1.0.0.7
+copy.v.1.0.0.V.6 turn.u.0.0.0.0 copy.y.1.0.1.V.7 copy.y.1.0.0.S.7 lmm.2.0.1 quant.v.1.0 copy.u.0.0.0.S.8 lmm.1.0.2
+quant.y.1.0 lexp.2.0 lmm.0.0.3 lmm.4.0.5 lexp.1.0 lmm.4.1.4 lexp.0.0 lmm.5.1.6 zgroup.0.0.V.9 lexp.4.0 lmm.3.1.7
+lmm.0.1.0 lexp.5.1 lmm.7.1.1 lmm.6.1.2 add.0.0.0.V turn.u.1.0.0.3 lexp.0.1 quant.z.0.0 lexp.6.1 turn.u.1.1.0.5
+zgroup.0.1.V.0 warmturn.u.1.1.1.6 lexp.7.1 lexp.4.1 warmturn.x.0.0.0.0 copy.u.1.1.0.V.2 add.1.1.1.G lexp.3.1
+turn.x.0.1.0.2 copy.u.1.1.1.V.2 lmm.7.0.1 copy.x.0.0.0.V.3 lmm.6.0.4 copy.x.0.1.0.S.4 lmm.1.1.5 quant.u.1.1
+turn.x.1.0.0.7 lexp.7.0 add.1.1.0.V lexp.1.1 warmturn.x.1.1.0.6 quant.z.0.1 copy.x.1.0.0.S.5 turn.x.1.0.1.0
+add.1.1.2.V lexp.6.0 lmm.3.0.2 copy.u.1.0.0.V.1 add.1.0.0.G copy.x.1.1.0.S.6 lmm.5.0.1 copy.x.1.0.1.V.5 lmm.2.1.5
+lexp.3.0 turn.u.0.1.1.7 add.0.1.1.V lexp.2.1 turn.u.1.0.1.4 quant.x.1.0 lexp.5.0 turn.u.0.1.0.3 add.0.0.1.V
+turn.x.0.1.1.6 copy.u.1.0.1.S.1 add.1.0.1.V turn.x.0.0.1.0 copy.u.0.1.1.S.7 add.0.0.2.V warmturn.u.0.0.1.2
+copy.x.0.1.1.S.4 quant.u.1.0 copy.x.0.0.1.S.3 turn.x.1.1.1.5 add.1.0.2.V zgroup.1.0.S.9 rowmean.0.0.1 quant.x.0.1
+quant.x.0.0 colsum copy.u.0.1.0.V.7 add.0.1.0.V rowmean.1.0.4 copy.u.0.0.1.S.8 quant.u.0.1 copy.x.1.1.1.S.6 grand.7
+quant.u.0.0 zgroup.1.1.S.2 rowmean.1.1.0 quant.x.1.1 kmm.4.0.6 shift quant.z.1.0 kmm.1.1.0 centre.5.1 add.0.1.2.G
+kmm.4.1.3 kexp.4.0 centre.7.1 kmm.0.1.2 kexp.1.1 centre.3.1 times_r.4.0.G kmm.3.1.5 kexp.4.1 centre.1.1 rowmean.0.1.0
+times_r.1.1.G kexp.0.1 centre.2.1 kexp.3.1 centre.6.1 times_r.4.1.G kmm.2.1.7 times_r.0.1.S centre.0.1 kmm.6.1.6
+times_r.3.1.S quant.z.1.1 kmm.5.1.0 kexp.2.1 centre.0.0 kmm.7.1.3 kexp.6.1 centre.4.1 times_r.2.1.G kmm.3.0.2 kexp.5.1
+centre.2.0 kmm.1.0.5 times_r.6.1.G kexp.7.1 centre.7.0 kmm.5.0.7 kexp.3.0 times_r.5.1.G centre.4.0 kmm.7.0.6 kexp.1.0
+centre.5.0 times_r.7.1.G kmm.0.0.4 times_r.3.0.S centre.1.0 kmm.6.0.0 kexp.7.0 product.0.1.1.0 kmm.2.0.3 kexp.0.0
+warm.2.10 kexp.6.0 product.1.1.0.5 kexp.2.0 kexp.5.0 product.0.1.0.0 times_r.6.0.S times_r.0.0.S product.1.1.1.5
+times_r.1.0.S times_r.5.0.S quant.a.0.1 times_r.2.0.S quant.a.1.1 times_r.7.0.S centre.6.0 omm.1.0.1.2 centre.3.0
+product.1.0.1.1 omm.1.0.0.5 ocopy.1.0.1.S product.0.0.0.4 omm.1.1.1.6 ocopy.1.0.0.S omm.1.0.3.4 product.0.0.1.4
+ocopy.1.1.1.S omm.1.1.0.0 ocopy.1.0.3.S omm.1.0.2.3 product.1.0.0.1 ocopy.1.1.0.S omm.1.1.3.7 ocopy.1.0.2.S
+omm.1.1.2.1 quant.a.0.0 ocopy.1.1.3.S quant.a.1.0 ocopy.1.1.2.S oround.1.0.1.V.3 oround.1.0.0.S.3 omm.0.1.0.2
+oround.1.1.1.V.7 omm.0.0.0.5 oquant.1.0.1 omm.0.0.1.6 ocopy.0.1.0.V ocopy.0.0.0.S omm.0.1.1.4 oquant.1.1.1
+oquant.1.0.0 ocopy.0.0.1.S omm.0.1.2.0 oround.1.1.0.V.7 ocopy.0.1.1.S omm.0.0.3.3 ocopy.0.1.2.V omm.0.0.2.7
+ocopy.0.0.3.S oquant.1.1.0 omm.0.1.3.1 ocopy.0.0.2.V ocopy.0.1.3.S oround.0.0.1.V.8 oround.0.0.0.S.8 oround.0.1.1.V.6
+oquant.0.0.1 oround.0.1.0.S.6 oquant.0.1.1 oquant.0.0.0 oquant.0.1.0
+"""
 
 
 def tile_hsicexpkernelgrad_x1_kernel(tc, x, u, y, v, r, z, out_0, out_1, out_2):
     nc = tc.nc
     with ExitStack() as ctx:
         const = ctx.enter_context(tc.tile_pool(name="const", bufs=1))
-        raw = ctx.enter_context(tc.tile_pool(name="raw", bufs=1))
-        grp = ctx.enter_context(tc.tile_pool(name="grp", bufs=1))
+        wide = ctx.enter_context(tc.tile_pool(name="wide", bufs=1))
+        buffers = ctx.enter_context(tc.tile_pool(name="buffers", bufs=1))
         codes = ctx.enter_context(tc.tile_pool(name="codes", bufs=1))
         big = ctx.enter_context(tc.tile_pool(name="big", bufs=1))
         psum = ctx.enter_context(tc.psum_pool(name="psum", bufs=1))
+        ctx.enter_context(tc.manual_schedule())
 
-        ident = const.tile([P, P], F32, name="ident")
-        make_identity(nc, ident[:])
-        ones_mean = const.tile([P, P], F32, name="ones_mean")
-        nc.gpsimd.memset(ones_mean[:], 1.0 / 1024)
-        ones_grand = const.tile([P, P], F32, name="ones_grand")
-        nc.gpsimd.memset(ones_grand[:], 1.0 / (1024 * 1024))
-        dummy = const.tile([P, GROUP], BF16, name="dummy")
-        nc.vector.memset(dummy[:], 0.0)
-        warm = const.tile([P, 1], F32, name="warm")
-        nc.vector.memset(warm[:], 0.0)
-        warm_out = const.tile([P, 1], F32, name="warm_out")
-        nc.scalar.activation(out=warm_out[:], in_=warm[:], func=ACT.Exp)
-        r_bf = const.tile([P, 2, PACK], BF16, name="r_bf")
-        nc.gpsimd.dma_start(out=r_bf[:], in_=r.rearrange("(g p t) -> p g t", p=P, t=PACK))
-        r_sb = const.tile([P, 8], F32, name="r_sb")
-        nc.gpsimd.tensor_copy(out=r_sb[:], in_=r_bf[:].rearrange("p g t -> p (g t)"))
-        sums = const.tile([P, 2, 8], F32, name="sums")
+        zeros = const.tile([P, GROUP], BF16, name="zeros")
+        nc.vector.memset(zeros[:], 0.0)
+        table_in = const.tile([P, 1], F32, name="table_in")
+        nc.vector.memset(table_in[:], 0.0)
+        table_out = const.tile([P, 1], F32, name="table_out")
+        nc.scalar.activation(out=table_out[:], in_=table_in[:], func=ACT.Exp)
+        identity = const.tile([P, P], F32, name="identity")
+        make_identity(nc, identity[:])
+        over_rows = const.tile([P, P], F32, name="over_rows")
+        nc.gpsimd.memset(over_rows[:], 1.0 / M)
+        over_all = const.tile([P, P], F32, name="over_all")
+        nc.gpsimd.memset(over_all[:], 1.0 / (N * M))
+        r_raw = const.tile([P, 2, PACK], BF16, name="r_raw")
+        nc.gpsimd.dma_start(out=r_raw[:], in_=r.rearrange("(g p t) -> p g t", p=P, t=PACK))
+        r_col = const.tile([P, TILES], F32, name="r_col")
+        nc.gpsimd.tensor_copy(out=r_col[:], in_=r_raw[:].rearrange("p g t -> p (g t)"))
+        l_sums = const.tile([P, 2, TILES], F32, name="l_sums")
+        col_sum = const.tile([P, TILES], F32, name="col_sum")
+        col_total = const.tile([P, 1], F32, name="col_total")
+        offset = const.tile([P, TILES], F32, name="offset")
 
-        raws = {}
+        source = {"x": x, "u": u, "y": y, "v": v, "z": z}
+        raw = {}
+        for g in range(2):
+            for name in "yv":
+                raw[name, g] = buffers.tile([P, PACK, E], BF16, name="raw_" + name, tag="buffer%d" % (2 * "yv".index(name) + g), align_bytes=64)
+            for name in "uxz":
+                raw[name, g] = wide.tile([P, PACK, D], BF16, name="raw_" + name, tag="wide%d" % (2 * "uxz".index(name) + g))
+        for piece in LOADS.split():
+            name, g = piece[0], int(piece[1])
+            slots = {"a": slice(0, 2), "b": slice(2, 4), "": slice(0, 4)}[piece[2:]]
+            rows = source[name][g * GROUP:(g + 1) * GROUP, :].rearrange("(m t) k -> m t k", t=PACK)
+            nc.sync.dma_start(out=raw[name, g][:, slots, :], in_=rows[:, slots, :])
 
-        def load_rows(name, src, g, pieces):
-            k_len = src.shape[1]
-            t_ = raw.tile([P, PACK, k_len], BF16, name="raw_%s%d" % (name, g), tag="short" if k_len == E else "wide", bufs=4 if k_len == E else 6)
-            rows = src[g * GROUP:(g + 1) * GROUP, :].rearrange("(m t) k -> m t k", t=PACK)
-            w = PACK // pieces
-            for b in range(pieces):
-                nc.sync.dma_start(out=t_[:, b * w:(b + 1) * w, :], in_=rows[:, b * w:(b + 1) * w, :])
-            raws[name, g] = t_
+        l_sb = [big.tile([P, TILES, GROUP], F32, name="l_sb%d" % ih) for ih in range(2)]
+        k_sb = [big.tile([P, TILES, GROUP], F32, name="k_sb%d" % ih) for ih in range(2)]
+        partial = [big.tile([P, TILES // 2, GROUP], F32, name="partial%d" % ih) for ih in range(2)]
+        out_codes = [codes.tile([P, COLS], U32, name="out_codes%d" % ih, align_bytes=64) for ih in range(2)]
+        out_scales = [codes.tile([P, COLS], U8, name="out_scales%d" % ih, align_bytes=64) for ih in range(2)]
+        words = {}
+        scales = {}
+        grouped = {}
+        banks = {}
+        result = {}
+        stored = []
+        quantised = []
 
-        load_rows("y", y, 0, 2)
-        load_rows("v", v, 0, 1)
-        load_rows("v", v, 1, 1)
-        load_rows("y", y, 1, 1)
-        load_rows("u", u, 0, 2)
-        load_rows("u", u, 1, 2)
-        load_rows("x", x, 0, 2)
-        load_rows("z", z, 0, 2)
-        load_rows("z", z, 1, 2)
-        load_rows("x", x, 1, 2)
-
-        turn_ring = [0, 1, 2, 3, 4]
-        acc_ring = [5, 6, 7]
-        out_ring = [0, 1, 2, 5, 6, 7, 3, 4]
-
-        def next_bank(ring):
-            i = ring[0]
-            ring.remove(i)
-            ring.append(i)
+        def new_bank(i):
             return psum.tile([P, GROUP], F32, name="bank", tag="bank%d" % i)
 
-        def turn_bank():
-            return next_bank(turn_ring)[:].rearrange("p (a e r) -> p a e r", a=2, e=2)
-
-        code = {}
-        plane = {}
-        grouped = {}
-
-        def turn(name, g, h, b):
-            words = raws[name, g][:].rearrange("m t k -> m (t k)").bitcast(F32)
-            per_row = (E if name in "yv" else D) // 2
-            bank = turn_bank()
-            for a in range(2):
-                base = (2 * b + a) * per_row + 256 * h
-                for e in range(2):
-                    nc.tensor.transpose(bank[:, a, e, :], words[:, base + e:base + 256:2], ident[:])
-            return bank
-
-        def copy_out(bank, name, g, h, b, eng):
-            key = (name, g, h)
+        def new_grouped(key, buffer):
             if key not in grouped:
-                grouped[key] = grp.tile([P, GROUP, PACK], BF16, name="grouped", tag="grouped", bufs=6, align_bytes=64)
-            dst = grouped[key][:].rearrange("p r k -> p (r k)").bitcast(F32)
-            dst = dst.rearrange("p (b a r e) -> p b a r e", b=2, a=2, e=2)[:, b]
-            src = bank.rearrange("p a e r -> p a r e")
-            if eng == "V":
+                grouped[key] = buffers.tile([P, GROUP, PACK], BF16, name="grouped", tag="buffer%d" % buffer, align_bytes=64)
+            return grouped[key]
+
+        def keep_clock_up(bank, count):
+            for repeat in range(count):
+                nc.tensor.matmul(bank[:], lhsT=zeros[:, 0:P], rhs=zeros[:], start=True, stop=True)
+
+        def warm(i, count):
+            keep_clock_up(new_bank(i), count)
+
+
+        def turn(name, g, h, b, i, warmers=0):
+            pairs = raw[name, g][:].rearrange("m t k -> m (t k)").bitcast(F32)
+            row_pairs = source[name].shape[1] // 2
+            bank = new_bank(i)
+            banks["turn", name, g, h, b] = bank
+            keep_clock_up(bank, warmers)
+            turned = bank[:].rearrange("p (slot e m) -> p slot e m", slot=2, e=2)
+            for slot in range(2):
+                first = (2 * b + slot) * row_pairs + (GROUP // 2) * h
+                for e in range(2):
+                    nc.tensor.transpose(turned[:, slot, e, :], pairs[:, first + e:first + GROUP // 2:2], identity[:])
+
+        def warmturn(name, g, h, b, i):
+            turn(name, g, h, b, i, 1)
+
+        def copy(name, g, h, b, engine, buffer):
+            dst = new_grouped((name, g, h), buffer)[:].rearrange("p r t -> p (r t)").bitcast(F32)
+            dst = dst.rearrange("p (b slot m e) -> p b slot m e", b=2, slot=2, e=2)[:, b]
+            src = banks["turn", name, g, h, b][:].rearrange("p (slot e m) -> p slot m e", slot=2, e=2)
+            if engine == "V":
                 nc.vector.tensor_copy(out=dst, in_=src)
             else:
                 nc.scalar.copy(out=dst, in_=src)
 
-        def quantize(key, src):
-            c_ = codes.tile([P, GROUP], U32, name="c_%s%d%d" % key, align_bytes=64)
-            s_ = codes.tile([P, GROUP], U8, name="s_%s%d%d" % key, align_bytes=64)
-            nc.vector.quantize_mx(out=c_[:].bitcast(FP8X4), scales=s_[:], in_=src[:].rearrange("p r k -> p (r k)"))
-            code[key] = c_
-            plane[key] = s_
+        def zgroup(g, n, engine, buffer):
+            dst = new_grouped(("z", g, n), buffer)[:].rearrange("p (c i) t -> p c t i", i=4)
+            src = raw["z", g][:, :, n * GROUP:(n + 1) * GROUP].rearrange("p t (c i) -> p c t i", i=4)
+            if engine == "V":
+                nc.vector.tensor_copy(out=dst, in_=src)
+            else:
+                nc.scalar.copy(out=dst, in_=src)
 
-        def mx(bank, lkey, lcols, rkey, rcols, start, stop):
+        def quant(name, g, h):
+            key = (name, g, h)
+            words[key] = codes.tile([P, GROUP], U32, name="words", tag="c_%s%d%d" % key, align_bytes=64)
+            scales[key] = codes.tile([P, GROUP], U8, name="scales", tag="s_%s%d%d" % key, align_bytes=64)
+            nc.vector.quantize_mx(out=words[key][:].bitcast(FP8X4), scales=scales[key][:], in_=grouped[key][:].rearrange("p r t -> p (r t)"))
+
+        def mx(bank, stationary, t, moving, start, stop):
+            cols = slice(t * P, (t + 1) * P)
             nc.tensor.matmul_mx(
-                out=bank[:], lhsT=code[lkey][:, lcols].bitcast(FP8X4), lhsT_scale=plane[lkey][:, lcols],
-                rhs=code[rkey][:, rcols].bitcast(FP8X4), rhs_scale=plane[rkey][:, rcols], start=start, stop=stop)
+                out=bank[:], lhsT=words[stationary][:, cols].bitcast(FP8X4), lhsT_scale=scales[stationary][:, cols],
+                rhs=words[moving][:].bitcast(FP8X4), rhs_scale=scales[moving][:], start=start, stop=stop)
 
-        full = slice(0, GROUP)
 
-        l_sb = [big.tile([P, 8, GROUP], F32, name="l_sb%d" % ih) for ih in range(2)]
-        k_sb = [big.tile([P, 8, GROUP], F32, name="k_sb%d" % ih) for ih in range(2)]
-        pair = [big.tile([P, 4, GROUP], F32, name="pair%d" % ih) for ih in range(2)]
+        def lmm(jt, ih, i):
+            banks["l", jt, ih] = new_bank(i)
+            mx(banks["l", jt, ih], ("v", jt // PACK, 0), jt % PACK, ("y", ih, 0), True, True)
 
-        def acc_bank():
-            return next_bank(acc_ring)
+        def lexp(jt, ih):
+            nc.scalar.activation(out=l_sb[ih][:, jt, :], in_=banks["l", jt, ih][:], func=ACT.Exp, scale=1.0 / math.sqrt(E),
+                                 accum_out=l_sums[:, ih, jt:jt + 1])
 
-        def l_mm(jt, ih):
-            g, t = divmod(jt, 4)
-            bank = acc_bank()
-            mx(bank, ("v", g, 0), slice(t * P, (t + 1) * P), ("y", ih, 0), full, True, True)
-            return bank
+        def add(ih, q, a, engine):
+            lo, hi = partial[ih][:, 2 * q, :], partial[ih][:, 2 * q + 1, :]
+            if a < 2:
+                out, in0, in1 = (lo, hi)[a], l_sb[ih][:, 4 * q + 2 * a, :], l_sb[ih][:, 4 * q + 2 * a + 1, :]
+            else:
+                out, in0, in1 = lo, lo, hi
+            (nc.gpsimd if engine == "G" else nc.vector).tensor_tensor(out=out, in0=in0, in1=in1, op=ALU.add)
 
-        def l_exp(bank, jt, ih):
-            nc.scalar.activation(out=l_sb[ih][:, jt, :], in_=bank[:], func=ACT.Exp, scale=1.0 / math.sqrt(E),
-                                 accum_out=sums[:, ih, jt:jt + 1])
+        def rowmean(ih, q, i):
+            if q == 0:
+                banks["mean", ih] = new_bank(i)
+            nc.tensor.matmul(banks["mean", ih][:], lhsT=over_rows[:], rhs=partial[ih][:, 2 * q, :], start=q == 0, stop=q == 1)
 
-        def pair_add(q, ih):
-            nc.vector.tensor_tensor(out=pair[ih][:, q, :], in0=l_sb[ih][:, 2 * q, :], in1=l_sb[ih][:, 2 * q + 1, :], op=ALU.add)
+        def colsum():
+            nc.vector.tensor_tensor(out=col_sum[:], in0=l_sums[:, 0, :], in1=l_sums[:, 1, :], op=ALU.add)
+            nc.vector.reduce_sum(out=col_total[:], in_=col_sum[:], axis=AX.X)
 
-        def k_mm(jt, ih):
-            g, t = divmod(jt, 4)
-            bank = acc_bank()
-            for h in range(2):
-                mx(bank, ("u", g, h), slice(t * P, (t + 1) * P), ("x", ih, h), full, h == 0, h == 1)
-            return bank
+        def grand(i):
+            banks["grand"] = new_bank(i)
+            nc.tensor.matmul(banks["grand"][:, 0:1], lhsT=over_all[:], rhs=col_total[:], start=True, stop=True)
 
-        def k_exp(bank, jt, ih):
-            nc.scalar.activation(out=k_sb[ih][:, jt, :], in_=bank[:], func=ACT.Exp, scale=1.0 / math.sqrt(D))
-
-        def k_r(jt, ih, eng):
-            if eng == "S":
-                nc.scalar.activation(out=k_sb[ih][:, jt, :], in_=k_sb[ih][:, jt, :], func=ACT.Copy, scale=r_sb[:, jt:jt + 1])
-                return
-            (nc.gpsimd if eng == "G" else nc.vector).tensor_scalar(out=k_sb[ih][:, jt, :], in0=k_sb[ih][:, jt, :], scalar1=r_sb[:, jt:jt + 1], scalar2=0.0,
-                                    op0=ALU.mult, op1=ALU.add)
-
-        mean = {}
-
-        def keep_warm(count):
-            bank = psum.tile([P, GROUP], F32, name="bank", tag="bank7")
-            for i in range(count):
-                nc.tensor.matmul(bank[:], lhsT=dummy[:, 0:P], rhs=dummy[:], start=True, stop=True)
-
-        def mean_mm(ih):
-            mean[ih] = psum.tile([P, GROUP], F32, name="mean", tag="bank%d" % (3 + ih))
-            for q in range(0, 4, 2):
-                nc.tensor.matmul(mean[ih][:], lhsT=ones_mean[:], rhs=pair[ih][:, q, :], start=q == 0, stop=q == 2)
-
-        def quad_add(q, ih):
-            nc.vector.tensor_tensor(out=pair[ih][:, 2 * q, :], in0=pair[ih][:, 2 * q, :], in1=pair[ih][:, 2 * q + 1, :], op=ALU.add)
-
-        shift = const.tile([P, 8], F32, name="shift")
-
-        def column_means():
-            col = const.tile([P, 8], F32, name="col")
-            nc.vector.tensor_tensor(out=col[:], in0=sums[:, 0, :], in1=sums[:, 1, :], op=ALU.add)
-            tot = const.tile([P, 1], F32, name="tot")
-            nc.vector.reduce_sum(out=tot[:], in_=col[:], axis=AX.X)
-            bank = next_bank(acc_ring)
-            grand = bank[:, 0:1]
-            nc.tensor.matmul(grand, lhsT=ones_grand[:], rhs=tot[:], start=True, stop=True)
-            nc.vector.tensor_scalar(out=shift[:], in0=col[:], scalar1=-1.0 / 1024, scalar2=grand, op0=ALU.mult, op1=ALU.add)
+        def shift():
+            nc.vector.tensor_scalar(out=offset[:], in0=col_sum[:], scalar1=-1.0 / N, scalar2=banks["grand"][:, 0:1], op0=ALU.mult, op1=ALU.add)
 
         def centre(jt, ih):
-            nc.vector.scalar_tensor_tensor(out=l_sb[ih][:, jt, :], in0=l_sb[ih][:, jt, :], scalar=shift[:, jt:jt + 1],
-                                           in1=mean[ih][:], op0=ALU.add, op1=ALU.subtract)
+            nc.vector.scalar_tensor_tensor(out=l_sb[ih][:, jt, :], in0=l_sb[ih][:, jt, :], scalar=offset[:, jt:jt + 1],
+                                           in1=banks["mean", ih][:], op0=ALU.add, op1=ALU.subtract)
 
-        def product(jg, ih, part, parts):
-            key = ("a", jg, ih)
-            if key not in grouped:
-                grouped[key] = grp.tile([P, GROUP, PACK], BF16, name="grouped", tag="grouped", bufs=6, align_bytes=64)
-            w = GROUP // parts
-            cols = slice(part * w, (part + 1) * w)
+
+        def kmm(jt, ih, i):
+            banks["k", jt, ih] = new_bank(i)
+            for h in range(2):
+                mx(banks["k", jt, ih], ("u", jt // PACK, h), jt % PACK, ("x", ih, h), h == 0, h == 1)
+
+        def kexp(jt, ih):
+            nc.scalar.activation(out=k_sb[ih][:, jt, :], in_=banks["k", jt, ih][:], func=ACT.Exp, scale=1.0 / math.sqrt(D))
+
+        def times_r(jt, ih, engine):
+            tile_k, factor = k_sb[ih][:, jt, :], r_col[:, jt:jt + 1]
+            if engine == "S":
+                nc.scalar.activation(out=tile_k, in_=tile_k, func=ACT.Copy, scale=factor)
+            elif engine == "V":
+                nc.vector.tensor_scalar(out=tile_k, in0=tile_k, scalar1=factor, scalar2=None, op0=ALU.mult)
+            else:
+                nc.gpsimd.tensor_scalar(out=tile_k, in0=tile_k, scalar1=factor, scalar2=0.0, op0=ALU.mult, op1=ALU.add)
+
+
+        def product(g, ih, part, buffer):
+            cols = slice(part * HALF, (part + 1) * HALF)
+            four = slice(PACK * g, PACK * (g + 1))
             nc.vector.tensor_tensor(
-                out=grouped[key][:, cols, :].rearrange("p (c i) t -> p c t i", i=4),
-                in0=l_sb[ih][:, 4 * jg:4 * jg + 4, cols].rearrange("p t (c i) -> p c t i", i=4),
-                in1=k_sb[ih][:, 4 * jg:4 * jg + 4, cols].rearrange("p t (c i) -> p c t i", i=4), op=ALU.mult)
+                out=new_grouped(("a", g, ih), buffer)[:, cols, :].rearrange("p (c i) t -> p c t i", i=4),
+                in0=l_sb[ih][:, four, cols].rearrange("p t (c i) -> p c t i", i=4),
+                in1=k_sb[ih][:, four, cols].rearrange("p t (c i) -> p c t i", i=4), op=ALU.mult)
 
-        def z_interleave(g, n, eng):
-            key = ("z", g, n)
-            grouped[key] = grp.tile([P, GROUP, PACK], BF16, name="grouped", tag="grouped", bufs=6, align_bytes=64)
-            dst = grouped[key][:].rearrange("p (c i) t -> p c t i", i=4)
-            src = raws["z", g][:, :, n * GROUP:(n + 1) * GROUP].rearrange("p t (c i) -> p c t i", i=4)
-            if eng == "V":
-                nc.vector.tensor_copy(out=dst, in_=src)
-            else:
-                nc.scalar.copy(out=dst, in_=src)
-
-        def q_(key):
-            quantize(key, grouped[key])
-
-        res = {}
-        resg = {}
-
-        def out_mm(ih, n, t):
-            flat = next_bank(out_ring)[:]
+        def omm(ih, n, t, i):
+            banks["o", ih, n, t] = new_bank(i)
             for g in range(2):
-                nc.tensor.matmul_mx(
-                    out=flat, lhsT=code["a", g, ih][:, t * P:(t + 1) * P].bitcast(FP8X4), lhsT_scale=plane["a", g, ih][:, t * P:(t + 1) * P],
-                    rhs=code["z", g, n][:].bitcast(FP8X4), rhs_scale=plane["z", g, n][:], start=g == 0, stop=g == 1)
-            return flat
+                mx(banks["o", ih, n, t], ("a", g, ih), t, ("z", g, n), g == 0, g == 1)
 
-        def out_copy(flat, ih, n, t, eng):
-            if (ih, n) not in res:
-                res[ih, n] = raw.tile([P, PACK, GROUP], F32, name="res", tag="wide", bufs=6)
-            dst = res[ih, n][:, t, :]
-            if eng == "V":
-                nc.vector.tensor_scalar(out=dst, in0=flat, scalar1=1.0 / 32, scalar2=None, op0=ALU.mult)
+        def ocopy(ih, n, t, engine):
+            if (ih, n) not in result:
+                result[ih, n] = wide.tile([P, PACK, GROUP], F32, name="result", tag="wide%d" % (2 * ih + n))
+            dst, src = result[ih, n][:, t, :], banks["o", ih, n, t][:]
+            if engine == "V":
+                nc.vector.tensor_scalar(out=dst, in0=src, scalar1=1.0 / math.sqrt(M), scalar2=None, op0=ALU.mult)
             else:
-                nc.scalar.activation(out=dst, in_=flat, func=ACT.Copy, scale=1.0 / 32)
+                nc.scalar.activation(out=dst, in_=src, func=ACT.Copy, scale=1.0 / math.sqrt(M))
+            stored.append((ih, n, t // 2))
+            if stored.count((ih, n, t // 2)) == 2:
+                slots = slice(t // 2 * 2, t // 2 * 2 + 2)
+                rows = out_0[ih * GROUP:(ih + 1) * GROUP, n * GROUP:(n + 1) * GROUP].rearrange("(m t) c -> m t c", t=PACK)
+                nc.sync.dma_start(out=rows[:, slots, :], in_=result[ih, n][:, slots, :])
 
-        def out_store(ih, n, ts):
-            nc.sync.dma_start(
-                out=out_0[ih * GROUP:(ih + 1) * GROUP, n * GROUP:(n + 1) * GROUP].rearrange("(m t) p -> m t p", t=PACK)[:, ts, :],
-                in_=res[ih, n][:, ts, :])
+        def oround(ih, n, part, engine, buffer):
+            cols = slice(part * HALF, (part + 1) * HALF)
+            (nc.scalar.copy if engine == "S" else nc.vector.tensor_copy)(
+                out=new_grouped(("o", ih, n), buffer)[:, cols, :].rearrange("p (c i) t -> p c t i", i=4),
+                in_=result[ih, n][:, :, cols].rearrange("p t (c i) -> p c t i", i=4))
 
-        o_codes = [codes.tile([P, PCOLS], U32, name="o_codes%d" % ih, align_bytes=64) for ih in range(2)]
-        o_plane = [codes.tile([P, PCOLS], U8, name="o_plane%d" % ih, align_bytes=64) for ih in range(2)]
+        def oquant(ih, n, part):
+            cols = slice(part * HALF, (part + 1) * HALF)
+            to = slice(n * GROUP + part * HALF, n * GROUP + (part + 1) * HALF)
+            nc.vector.quantize_mx(out=out_codes[ih][:, to].bitcast(FP8X4), scales=out_scales[ih][:, to],
+                                  in_=grouped["o", ih, n][:, cols, :].rearrange("p c t -> p (c t)"))
+            quantised.append((ih, n))
+            if quantised.count((ih, n)) == 2:
+                both = slice(n * GROUP, (n + 1) * GROUP)
+                nc.sync.dma_start(out=out_1[ih][:, both, :].rearrange("p c t -> p (c t)").bitcast(I32), in_=out_codes[ih][:, both].bitcast(I32))
+                if quantised.count((ih, 1 - n)) == 2:
+                    for quadrant in range(4):
+                        nc.sync.dma_start(out=out_2[ih, 4 * quadrant:4 * quadrant + 4, :].bitcast(I32),
+                                          in_=out_scales[ih][32 * quadrant:32 * quadrant + 4, :].bitcast(I32))
 
-        def out_round(ih, n, eng="V", part=0, parts=1):
-            w = GROUP // parts
-            cols = slice(part * w, (part + 1) * w)
-            key = ("o", ih, n)
-            if key not in grouped:
-                grouped[key] = grp.tile([P, GROUP, PACK], BF16, name="grouped", tag="grouped", bufs=6, align_bytes=64)
-            (nc.scalar.copy if eng == "S" else nc.vector.tensor_copy)(
-                out=grouped[key][:, cols, :].rearrange("p (c i) t -> p c t i", i=4),
-                in_=res[ih, n][:, :, cols].rearrange("p t (c i) -> p c t i", i=4))
-
-        def out_quant(ih, n, part=0, parts=1):
-            w = GROUP // parts
-            cols = slice(part * w, (part + 1) * w)
-            gcols = slice(n * GROUP + part * w, n * GROUP + (part + 1) * w)
-            nc.vector.quantize_mx(out=o_codes[ih][:, gcols].bitcast(FP8X4), scales=o_plane[ih][:, gcols],
-                                  in_=grouped["o", ih, n][:, cols, :].rearrange("p n t -> p (n t)"))
-
-        def words_store(ih, first, last):
-            nc.sync.dma_start(out=out_1[ih][:, first:last, :].rearrange("p n t -> p (n t)").bitcast(I32),
-                              in_=o_codes[ih][:, first:last].bitcast(I32))
-
-        def plane_store(ih):
-            for q in range(4):
-                nc.sync.dma_start(out=out_2[ih, 4 * q:4 * q + 4, :].bitcast(I32), in_=o_plane[ih][32 * q:32 * q + 4, :].bitcast(I32))
-
-        def prep(name, g, h, engs):
-            for b in range(2):
-                copy_out(turn(name, g, h, b), name, g, h, b, engs[b])
-
-        keep_warm(5)
-        prep("y", 0, 0, "VS")
-        keep_warm(2)
-        q_(("y", 0, 0))
-        prep("v", 0, 0, "VS")
-        keep_warm(2)
-        q_(("v", 0, 0))
-        prep("v", 1, 0, "VS")
-        for jt in range(4):
-            l_exp(l_mm(jt, 0), jt, 0)
-        q_(("v", 1, 0))
-        prep("y", 1, 0, "VV")
-        for jt in range(4, 8):
-            l_exp(l_mm(jt, 0), jt, 0)
-        q_(("y", 1, 0))
-        pair_add(0, 0)
-        pair_add(1, 0)
-        for s in range(4):
-            g, h = divmod(s, 2)
-            for jt in (2 * s, 2 * s + 1):
-                l_exp(l_mm(jt, 1), jt, 1)
-            prep("u", g, h, "VS")
-            if s < 2:
-                pair_add(2 + s, 0)
-            q_(("u", g, h))
-            quad_add(0, 0) if s == 0 else None
-            pair_add(s, 1)
-            if s == 1:
-                quad_add(1, 0)
-            if s == 2:
-                quad_add(0, 1)
-        prep("x", 0, 0, "SS")
-        prep("x", 0, 1, "SS")
-        q_(("x", 0, 0))
-        quad_add(1, 1)
-        q_(("x", 0, 1))
-        mean_mm(0)
-        z_interleave(0, 0, "V")
-        column_means()
-        for jt in range(8):
-            k_exp(k_mm(jt, 0), jt, 0)
-            k_r(jt, 0, "G")
-            centre(jt, 0)
-            if jt in (2, 5):
-                h = jt // 3
-                prep("x", 1, h, "SS")
-            if jt == 5:
-                q_(("x", 1, 0))
-        q_(("z", 0, 0))
-        q_(("x", 1, 1))
-        for n_ in (3, 4):
-            turn_ring.remove(n_)
-        mean_mm(1)
-        z_interleave(1, 0, "S")
-        product(0, 0, 0, 2)
-        product(0, 0, 1, 2)
-        product(1, 0, 0, 2)
-        q_(("a", 0, 0))
-        product(1, 0, 1, 2)
-        q_(("z", 1, 0))
-        for jt in range(8):
-            k_exp(k_mm(jt, 1), jt, 1)
-            k_r(jt, 1, "S")
-            centre(jt, 1)
-            if jt == 0:
-                q_(("a", 1, 0))
-        z_interleave(0, 1, "S")
-        product(0, 1, 0, 2)
-        for t in range(4):
-            out_copy(out_mm(0, 0, t), 0, 0, t, "S")
-        out_store(0, 0, slice(0, 4))
-        z_interleave(1, 1, "S")
-        q_(("z", 0, 1))
-        product(0, 1, 1, 2)
-        product(1, 1, 0, 2)
-        q_(("a", 0, 1))
-        q_(("z", 1, 1))
-        product(1, 1, 1, 2)
-        out_round(0, 0)
-        q_(("a", 1, 1))
-        for t in range(4):
-            out_copy(out_mm(0, 1, t), 0, 1, t, "S")
-        out_store(0, 1, slice(0, 4))
-        for t in range(4):
-            out_copy(out_mm(1, 0, t), 1, 0, t, "S")
-            if t % 2:
-                out_store(1, 0, slice(t - 1, t + 1))
-        out_round(0, 1)
-        out_quant(0, 0)
-        words_store(0, 0, 512)
-        out_quant(0, 1)
-        words_store(0, 512, 1024)
-        plane_store(0)
-        out_round(1, 0)
-        for t in range(4):
-            out_copy(out_mm(1, 1, t), 1, 1, t, "S")
-            if t % 2:
-                out_store(1, 1, slice(t - 1, t + 1))
-        out_quant(1, 0)
-        words_store(1, 0, 512)
-        out_round(1, 1, "V", 0, 2)
-        out_round(1, 1, "V", 1, 2)
-        out_quant(1, 1, 0, 2)
-        out_quant(1, 1, 1, 2)
-        words_store(1, 512, 1024)
-        plane_store(1)
+        steps = {"turn": turn, "warmturn": warmturn, "warm": warm, "copy": copy, "zgroup": zgroup, "quant": quant, "lmm": lmm,
+                 "lexp": lexp, "add": add, "rowmean": rowmean, "colsum": colsum, "grand": grand, "shift": shift,
+                 "centre": centre, "kmm": kmm, "kexp": kexp, "times_r": times_r, "product": product, "omm": omm,
+                 "ocopy": ocopy, "oround": oround, "oquant": oquant}
+        warm(7, HEAD_WARMERS)
+        for step in ORDER.split():
+            parts = step.split(".")
+            steps[parts[0]](*[part if part in "xyuvzaVSG" else int(part) for part in parts[1:]])

import math
from contextlib import ExitStack

import concourse.mybir as mybir
from concourse.masks import make_identity

N, M, D, E, COLS = 1024, 1024, 1024, 512, 1024
FLOPS = 2 * N * M * (D + E + COLS)

F32 = mybir.dt.float32
BF16 = mybir.dt.bfloat16
U32 = mybir.dt.uint32
I32 = mybir.dt.int32
U8 = mybir.dt.uint8
FP8X4 = mybir.dt.float8_e4m3fn_x4
ALU = mybir.AluOpType
ACT = mybir.ActivationFunctionType
AX = mybir.AxisListType

P = 128
PACK = 4
GROUP = P * PACK
TILES = 8
HALF = GROUP // 2
HEAD_WARMERS = 5

LOADS = "y0a y0b v0a v0b v1 y1 u0a u0b z0a z0b u1a u1b x0a x0b x1a x1b z1a z1b"

ORDER = """
warmturn.y.0.0.0.0 turn.y.0.0.1.1 copy.y.0.0.0.S.4 turn.v.0.0.0.2 copy.y.0.0.1.S.4 turn.v.0.0.1.3 copy.v.0.0.0.V.5
turn.v.1.0.0.4 copy.v.0.0.1.V.5 turn.v.1.0.1.5 quant.y.0.0 turn.y.1.0.1.6 quant.v.0.0 copy.v.1.0.1.S.6 turn.y.1.0.0.7
copy.v.1.0.0.V.6 turn.u.0.0.0.0 copy.y.1.0.1.V.7 copy.y.1.0.0.S.7 lmm.2.0.1 quant.v.1.0 copy.u.0.0.0.S.8 lmm.1.0.2
quant.y.1.0 lexp.2.0 lmm.0.0.3 lmm.4.0.5 lexp.1.0 lmm.4.1.4 lexp.0.0 lmm.5.1.6 zgroup.0.0.V.9 lexp.4.0 lmm.3.1.7
lmm.0.1.0 lexp.5.1 lmm.7.1.1 lmm.6.1.2 add.0.0.0.V turn.u.1.0.0.3 lexp.0.1 quant.z.0.0 lexp.6.1 turn.u.1.1.0.5
zgroup.0.1.V.0 warmturn.u.1.1.1.6 lexp.7.1 lexp.4.1 warmturn.x.0.0.0.0 copy.u.1.1.0.V.2 add.1.1.1.G lexp.3.1
turn.x.0.1.0.2 copy.u.1.1.1.V.2 lmm.7.0.1 copy.x.0.0.0.V.3 lmm.6.0.4 copy.x.0.1.0.S.4 lmm.1.1.5 quant.u.1.1
turn.x.1.0.0.7 lexp.7.0 add.1.1.0.V lexp.1.1 warmturn.x.1.1.0.6 quant.z.0.1 copy.x.1.0.0.S.5 turn.x.1.0.1.0
add.1.1.2.V lexp.6.0 lmm.3.0.2 copy.u.1.0.0.V.1 add.1.0.0.G copy.x.1.1.0.S.6 lmm.5.0.1 copy.x.1.0.1.V.5 lmm.2.1.5
lexp.3.0 turn.u.0.1.1.7 add.0.1.1.V lexp.2.1 turn.u.1.0.1.4 quant.x.1.0 lexp.5.0 turn.u.0.1.0.3 add.0.0.1.V
turn.x.0.1.1.6 copy.u.1.0.1.S.1 add.1.0.1.V turn.x.0.0.1.0 copy.u.0.1.1.S.7 add.0.0.2.V warmturn.u.0.0.1.2
copy.x.0.1.1.S.4 quant.u.1.0 copy.x.0.0.1.S.3 turn.x.1.1.1.5 add.1.0.2.V zgroup.1.0.S.9 rowmean.0.0.1 quant.x.0.1
quant.x.0.0 colsum copy.u.0.1.0.V.7 add.0.1.0.V rowmean.1.0.4 copy.u.0.0.1.S.8 quant.u.0.1 copy.x.1.1.1.S.6 grand.7
quant.u.0.0 zgroup.1.1.S.2 rowmean.1.1.0 quant.x.1.1 kmm.4.0.6 shift quant.z.1.0 kmm.1.1.0 centre.5.1 add.0.1.2.G
kmm.4.1.3 kexp.4.0 centre.7.1 kmm.0.1.2 kexp.1.1 centre.3.1 times_r.4.0.G kmm.3.1.5 kexp.4.1 centre.1.1 rowmean.0.1.0
times_r.1.1.G kexp.0.1 centre.2.1 kexp.3.1 centre.6.1 times_r.4.1.G kmm.2.1.7 times_r.0.1.S centre.0.1 kmm.6.1.6
times_r.3.1.S quant.z.1.1 kmm.5.1.0 kexp.2.1 centre.0.0 kmm.7.1.3 kexp.6.1 centre.4.1 times_r.2.1.G kmm.3.0.2 kexp.5.1
centre.2.0 kmm.1.0.5 times_r.6.1.G kexp.7.1 centre.7.0 kmm.5.0.7 kexp.3.0 times_r.5.1.G centre.4.0 kmm.7.0.6 kexp.1.0
centre.5.0 times_r.7.1.G kmm.0.0.4 times_r.3.0.S centre.1.0 kmm.6.0.0 kexp.7.0 product.0.1.1.0 kmm.2.0.3 kexp.0.0
warm.2.10 kexp.6.0 product.1.1.0.5 kexp.2.0 kexp.5.0 product.0.1.0.0 times_r.6.0.S times_r.0.0.S product.1.1.1.5
times_r.1.0.S times_r.5.0.S quant.a.0.1 times_r.2.0.S quant.a.1.1 times_r.7.0.S centre.6.0 omm.1.0.1.2 centre.3.0
product.1.0.1.1 omm.1.0.0.5 ocopy.1.0.1.S product.0.0.0.4 omm.1.1.1.6 ocopy.1.0.0.S omm.1.0.3.4 product.0.0.1.4
ocopy.1.1.1.S omm.1.1.0.0 ocopy.1.0.3.S omm.1.0.2.3 product.1.0.0.1 ocopy.1.1.0.S omm.1.1.3.7 ocopy.1.0.2.S
omm.1.1.2.1 quant.a.0.0 ocopy.1.1.3.S quant.a.1.0 ocopy.1.1.2.S oround.1.0.1.V.3 oround.1.0.0.S.3 omm.0.1.0.2
oround.1.1.1.V.7 omm.0.0.0.5 oquant.1.0.1 omm.0.0.1.6 ocopy.0.1.0.V ocopy.0.0.0.S omm.0.1.1.4 oquant.1.1.1
oquant.1.0.0 ocopy.0.0.1.S omm.0.1.2.0 oround.1.1.0.V.7 ocopy.0.1.1.S omm.0.0.3.3 ocopy.0.1.2.V omm.0.0.2.7
ocopy.0.0.3.S oquant.1.1.0 omm.0.1.3.1 ocopy.0.0.2.V ocopy.0.1.3.S oround.0.0.1.V.8 oround.0.0.0.S.8 oround.0.1.1.V.6
oquant.0.0.1 oround.0.1.0.S.6 oquant.0.1.1 oquant.0.0.0 oquant.0.1.0
"""


def tile_hsicexpkernelgrad_x1_kernel(tc, x, u, y, v, r, z, out_0, out_1, out_2):
    nc = tc.nc
    with ExitStack() as ctx:
        const = ctx.enter_context(tc.tile_pool(name="const", bufs=1))
        wide = ctx.enter_context(tc.tile_pool(name="wide", bufs=1))
        buffers = ctx.enter_context(tc.tile_pool(name="buffers", bufs=1))
        codes = ctx.enter_context(tc.tile_pool(name="codes", bufs=1))
        big = ctx.enter_context(tc.tile_pool(name="big", bufs=1))
        psum = ctx.enter_context(tc.psum_pool(name="psum", bufs=1))
        ctx.enter_context(tc.manual_schedule())

        zeros = const.tile([P, GROUP], BF16, name="zeros")
        nc.vector.memset(zeros[:], 0.0)
        table_in = const.tile([P, 1], F32, name="table_in")
        nc.vector.memset(table_in[:], 0.0)
        table_out = const.tile([P, 1], F32, name="table_out")
        nc.scalar.activation(out=table_out[:], in_=table_in[:], func=ACT.Exp)
        identity = const.tile([P, P], F32, name="identity")
        make_identity(nc, identity[:])
        over_rows = const.tile([P, P], F32, name="over_rows")
        nc.gpsimd.memset(over_rows[:], 1.0 / M)
        over_all = const.tile([P, P], F32, name="over_all")
        nc.gpsimd.memset(over_all[:], 1.0 / (N * M))
        r_raw = const.tile([P, 2, PACK], BF16, name="r_raw")
        nc.gpsimd.dma_start(out=r_raw[:], in_=r.rearrange("(g p t) -> p g t", p=P, t=PACK))
        r_col = const.tile([P, TILES], F32, name="r_col")
        nc.gpsimd.tensor_copy(out=r_col[:], in_=r_raw[:].rearrange("p g t -> p (g t)"))
        l_sums = const.tile([P, 2, TILES], F32, name="l_sums")
        col_sum = const.tile([P, TILES], F32, name="col_sum")
        col_total = const.tile([P, 1], F32, name="col_total")
        offset = const.tile([P, TILES], F32, name="offset")

        source = {"x": x, "u": u, "y": y, "v": v, "z": z}
        raw = {}
        for g in range(2):
            for name in "yv":
                raw[name, g] = buffers.tile([P, PACK, E], BF16, name="raw_" + name, tag="buffer%d" % (2 * "yv".index(name) + g), align_bytes=64)
            for name in "uxz":
                raw[name, g] = wide.tile([P, PACK, D], BF16, name="raw_" + name, tag="wide%d" % (2 * "uxz".index(name) + g))
        for piece in LOADS.split():
            name, g = piece[0], int(piece[1])
            slots = {"a": slice(0, 2), "b": slice(2, 4), "": slice(0, 4)}[piece[2:]]
            rows = source[name][g * GROUP:(g + 1) * GROUP, :].rearrange("(m t) k -> m t k", t=PACK)
            nc.sync.dma_start(out=raw[name, g][:, slots, :], in_=rows[:, slots, :])

        l_sb = [big.tile([P, TILES, GROUP], F32, name="l_sb%d" % ih) for ih in range(2)]
        k_sb = [big.tile([P, TILES, GROUP], F32, name="k_sb%d" % ih) for ih in range(2)]
        partial = [big.tile([P, TILES // 2, GROUP], F32, name="partial%d" % ih) for ih in range(2)]
        out_codes = [codes.tile([P, COLS], U32, name="out_codes%d" % ih, align_bytes=64) for ih in range(2)]
        out_scales = [codes.tile([P, COLS], U8, name="out_scales%d" % ih, align_bytes=64) for ih in range(2)]
        words = {}
        scales = {}
        grouped = {}
        banks = {}
        result = {}
        stored = []
        quantised = []

        def new_bank(i):
            return psum.tile([P, GROUP], F32, name="bank", tag="bank%d" % i)

        def new_grouped(key, buffer):
            if key not in grouped:
                grouped[key] = buffers.tile([P, GROUP, PACK], BF16, name="grouped", tag="buffer%d" % buffer, align_bytes=64)
            return grouped[key]

        def keep_clock_up(bank, count):
            for repeat in range(count):
                nc.tensor.matmul(bank[:], lhsT=zeros[:, 0:P], rhs=zeros[:], start=True, stop=True)

        def warm(i, count):
            keep_clock_up(new_bank(i), count)


        def turn(name, g, h, b, i, warmers=0):
            pairs = raw[name, g][:].rearrange("m t k -> m (t k)").bitcast(F32)
            row_pairs = source[name].shape[1] // 2
            bank = new_bank(i)
            banks["turn", name, g, h, b] = bank
            keep_clock_up(bank, warmers)
            turned = bank[:].rearrange("p (slot e m) -> p slot e m", slot=2, e=2)
            for slot in range(2):
                first = (2 * b + slot) * row_pairs + (GROUP // 2) * h
                for e in range(2):
                    nc.tensor.transpose(turned[:, slot, e, :], pairs[:, first + e:first + GROUP // 2:2], identity[:])

        def warmturn(name, g, h, b, i):
            turn(name, g, h, b, i, 1)

        def copy(name, g, h, b, engine, buffer):
            dst = new_grouped((name, g, h), buffer)[:].rearrange("p r t -> p (r t)").bitcast(F32)
            dst = dst.rearrange("p (b slot m e) -> p b slot m e", b=2, slot=2, e=2)[:, b]
            src = banks["turn", name, g, h, b][:].rearrange("p (slot e m) -> p slot m e", slot=2, e=2)
            if engine == "V":
                nc.vector.tensor_copy(out=dst, in_=src)
            else:
                nc.scalar.copy(out=dst, in_=src)

        def zgroup(g, n, engine, buffer):
            dst = new_grouped(("z", g, n), buffer)[:].rearrange("p (c i) t -> p c t i", i=4)
            src = raw["z", g][:, :, n * GROUP:(n + 1) * GROUP].rearrange("p t (c i) -> p c t i", i=4)
            if engine == "V":
                nc.vector.tensor_copy(out=dst, in_=src)
            else:
                nc.scalar.copy(out=dst, in_=src)

        def quant(name, g, h):
            key = (name, g, h)
            words[key] = codes.tile([P, GROUP], U32, name="words", tag="c_%s%d%d" % key, align_bytes=64)
            scales[key] = codes.tile([P, GROUP], U8, name="scales", tag="s_%s%d%d" % key, align_bytes=64)
            nc.vector.quantize_mx(out=words[key][:].bitcast(FP8X4), scales=scales[key][:], in_=grouped[key][:].rearrange("p r t -> p (r t)"))

        def mx(bank, stationary, t, moving, start, stop):
            cols = slice(t * P, (t + 1) * P)
            nc.tensor.matmul_mx(
                out=bank[:], lhsT=words[stationary][:, cols].bitcast(FP8X4), lhsT_scale=scales[stationary][:, cols],
                rhs=words[moving][:].bitcast(FP8X4), rhs_scale=scales[moving][:], start=start, stop=stop)


        def lmm(jt, ih, i):
            banks["l", jt, ih] = new_bank(i)
            mx(banks["l", jt, ih], ("v", jt // PACK, 0), jt % PACK, ("y", ih, 0), True, True)

        def lexp(jt, ih):
            nc.scalar.activation(out=l_sb[ih][:, jt, :], in_=banks["l", jt, ih][:], func=ACT.Exp, scale=1.0 / math.sqrt(E),
                                 accum_out=l_sums[:, ih, jt:jt + 1])

        def add(ih, q, a, engine):
            lo, hi = partial[ih][:, 2 * q, :], partial[ih][:, 2 * q + 1, :]
            if a < 2:
                out, in0, in1 = (lo, hi)[a], l_sb[ih][:, 4 * q + 2 * a, :], l_sb[ih][:, 4 * q + 2 * a + 1, :]
            else:
                out, in0, in1 = lo, lo, hi
            (nc.gpsimd if engine == "G" else nc.vector).tensor_tensor(out=out, in0=in0, in1=in1, op=ALU.add)

        def rowmean(ih, q, i):
            if q == 0:
                banks["mean", ih] = new_bank(i)
            nc.tensor.matmul(banks["mean", ih][:], lhsT=over_rows[:], rhs=partial[ih][:, 2 * q, :], start=q == 0, stop=q == 1)

        def colsum():
            nc.vector.tensor_tensor(out=col_sum[:], in0=l_sums[:, 0, :], in1=l_sums[:, 1, :], op=ALU.add)
            nc.vector.reduce_sum(out=col_total[:], in_=col_sum[:], axis=AX.X)

        def grand(i):
            banks["grand"] = new_bank(i)
            nc.tensor.matmul(banks["grand"][:, 0:1], lhsT=over_all[:], rhs=col_total[:], start=True, stop=True)

        def shift():
            nc.vector.tensor_scalar(out=offset[:], in0=col_sum[:], scalar1=-1.0 / N, scalar2=banks["grand"][:, 0:1], op0=ALU.mult, op1=ALU.add)

        def centre(jt, ih):
            nc.vector.scalar_tensor_tensor(out=l_sb[ih][:, jt, :], in0=l_sb[ih][:, jt, :], scalar=offset[:, jt:jt + 1],
                                           in1=banks["mean", ih][:], op0=ALU.add, op1=ALU.subtract)


        def kmm(jt, ih, i):
            banks["k", jt, ih] = new_bank(i)
            for h in range(2):
                mx(banks["k", jt, ih], ("u", jt // PACK, h), jt % PACK, ("x", ih, h), h == 0, h == 1)

        def kexp(jt, ih):
            nc.scalar.activation(out=k_sb[ih][:, jt, :], in_=banks["k", jt, ih][:], func=ACT.Exp, scale=1.0 / math.sqrt(D))

        def times_r(jt, ih, engine):
            tile_k, factor = k_sb[ih][:, jt, :], r_col[:, jt:jt + 1]
            if engine == "S":
                nc.scalar.activation(out=tile_k, in_=tile_k, func=ACT.Copy, scale=factor)
            elif engine == "V":
                nc.vector.tensor_scalar(out=tile_k, in0=tile_k, scalar1=factor, scalar2=None, op0=ALU.mult)
            else:
                nc.gpsimd.tensor_scalar(out=tile_k, in0=tile_k, scalar1=factor, scalar2=0.0, op0=ALU.mult, op1=ALU.add)


        def product(g, ih, part, buffer):
            cols = slice(part * HALF, (part + 1) * HALF)
            four = slice(PACK * g, PACK * (g + 1))
            nc.vector.tensor_tensor(
                out=new_grouped(("a", g, ih), buffer)[:, cols, :].rearrange("p (c i) t -> p c t i", i=4),
                in0=l_sb[ih][:, four, cols].rearrange("p t (c i) -> p c t i", i=4),
                in1=k_sb[ih][:, four, cols].rearrange("p t (c i) -> p c t i", i=4), op=ALU.mult)

        def omm(ih, n, t, i):
            banks["o", ih, n, t] = new_bank(i)
            for g in range(2):
                mx(banks["o", ih, n, t], ("a", g, ih), t, ("z", g, n), g == 0, g == 1)

        def ocopy(ih, n, t, engine):
            if (ih, n) not in result:
                result[ih, n] = wide.tile([P, PACK, GROUP], F32, name="result", tag="wide%d" % (2 * ih + n))
            dst, src = result[ih, n][:, t, :], banks["o", ih, n, t][:]
            if engine == "V":
                nc.vector.tensor_scalar(out=dst, in0=src, scalar1=1.0 / math.sqrt(M), scalar2=None, op0=ALU.mult)
            else:
                nc.scalar.activation(out=dst, in_=src, func=ACT.Copy, scale=1.0 / math.sqrt(M))
            stored.append((ih, n, t // 2))
            if stored.count((ih, n, t // 2)) == 2:
                slots = slice(t // 2 * 2, t // 2 * 2 + 2)
                rows = out_0[ih * GROUP:(ih + 1) * GROUP, n * GROUP:(n + 1) * GROUP].rearrange("(m t) c -> m t c", t=PACK)
                nc.sync.dma_start(out=rows[:, slots, :], in_=result[ih, n][:, slots, :])

        def oround(ih, n, part, engine, buffer):
            cols = slice(part * HALF, (part + 1) * HALF)
            (nc.scalar.copy if engine == "S" else nc.vector.tensor_copy)(
                out=new_grouped(("o", ih, n), buffer)[:, cols, :].rearrange("p (c i) t -> p c t i", i=4),
                in_=result[ih, n][:, :, cols].rearrange("p t (c i) -> p c t i", i=4))

        def oquant(ih, n, part):
            cols = slice(part * HALF, (part + 1) * HALF)
            to = slice(n * GROUP + part * HALF, n * GROUP + (part + 1) * HALF)
            nc.vector.quantize_mx(out=out_codes[ih][:, to].bitcast(FP8X4), scales=out_scales[ih][:, to],
                                  in_=grouped["o", ih, n][:, cols, :].rearrange("p c t -> p (c t)"))
            quantised.append((ih, n))
            if quantised.count((ih, n)) == 2:
                both = slice(n * GROUP, (n + 1) * GROUP)
                nc.sync.dma_start(out=out_1[ih][:, both, :].rearrange("p c t -> p (c t)").bitcast(I32), in_=out_codes[ih][:, both].bitcast(I32))
                if quantised.count((ih, 1 - n)) == 2:
                    for quadrant in range(4):
                        nc.sync.dma_start(out=out_2[ih, 4 * quadrant:4 * quadrant + 4, :].bitcast(I32),
                                          in_=out_scales[ih][32 * quadrant:32 * quadrant + 4, :].bitcast(I32))

        steps = {"turn": turn, "warmturn": warmturn, "warm": warm, "copy": copy, "zgroup": zgroup, "quant": quant, "lmm": lmm,
                 "lexp": lexp, "add": add, "rowmean": rowmean, "colsum": colsum, "grand": grand, "shift": shift,
                 "centre": centre, "kmm": kmm, "kexp": kexp, "times_r": times_r, "product": product, "omm": omm,
                 "ocopy": ocopy, "oround": oround, "oquant": oquant}
        warm(7, HEAD_WARMERS)
        for step in ORDER.split():
            parts = step.split(".")
            steps[parts[0]](*[part if part in "xyuvzaVSG" else int(part) for part in parts[1:]])
